import numpy as np
import ml_dtypes


def mxq(x, axis, fmt="e4m3"):
    dtype, down = {"e4m3": (ml_dtypes.float8_e4m3fn, 7), "e5m2": (ml_dtypes.float8_e5m2, 14)}[fmt]
    v = np.moveaxis(np.asarray(x, np.float32).astype(ml_dtypes.bfloat16).astype(np.float64), axis, -1)
    blocks = v.reshape(v.shape[:-1] + (-1, 32))
    amax = np.abs(blocks).max(-1, keepdims=True)
    byte = np.maximum(np.where(amax > 0, np.frexp(amax)[1] - 1 + 127, 0) - down, 1)
    scale = np.exp2(byte - 127.0)
    codes = (blocks / scale).astype(np.float32).astype(dtype).astype(np.float64)
    return np.moveaxis((codes * scale).reshape(v.shape), -1, axis)


WIDE = False


def mx_kscale(k, group=512):
    if not WIDE:
        return np.ones(k)
    levels = np.array([10, -10, 5, -5, 0])
    if group != 512:
        return np.exp2(np.random.permutation(np.resize(levels, k // group))).repeat(group)
    if k % 512:
        return np.exp2(np.random.permutation(np.resize(levels, k // 32))).repeat(32)
    a = np.empty((k // 512, 16))
    for p in range(k // 512):
        a[p, :8] = np.random.permutation(np.resize(levels, 8))
        for g in range(8):
            far = levels[np.abs(levels - a[p, g]) >= 10]
            a[p, g + 8] = far[np.random.randint(len(far))]
    return np.exp2(a.ravel()).repeat(32)


def f64(x):
    return np.asarray(x).astype(np.float64)


G, D, K, M, N = 4, 256, 512, 128, 512


def setup_inputs():
    n = np.random.standard_normal
    s = mx_kscale(D, 0)[:, None]
    u = mx_kscale(K)[:, None]
    return {
        "x": (n((G, D, N)) * s).astype(np.float32),
        "w1": (n((G, D, K)) / np.sqrt(D) / s).astype(np.float32),
        "hs": (np.random.uniform(0.5, 2.0, (G, K, 1)) * u).astype(np.float32),
        "w2": (n((G, K, M)) / np.sqrt(K) / u).astype(np.float32),
    }


def reference(x, w1, hs, w2):
    xq = mxq(f64(x), 1, "e4m3")
    h = mxq(f64(w1), 1, "e4m3").transpose(0, 2, 1) @ xq
    h = (h) * f64(hs)
    y = mxq(f64(w2), 1, "e4m3").transpose(0, 2, 1) @ mxq(h, 1, "e4m3")
    return y

@@ -1,0 +1,241 @@
+from contextlib import ExitStack
+
+import concourse.mybir as mybir
+
+G, D, K, M, N = 4, 256, 512, 128, 512
+FLOPS = 2 * G * D * K * N + 2 * G * K * M * N
+
+F32 = mybir.dt.float32
+BF16 = mybir.dt.bfloat16
+U32 = mybir.dt.uint32
+U8 = mybir.dt.uint8
+FP8X4 = mybir.dt.float8_e4m3fn_x4
+MULT = mybir.AluOpType.mult
+COPY = mybir.ActivationFunctionType.Copy
+
+P = 128
+ROWS = 64
+PACK = 4
+CH = 128
+W1_VECTOR_SHARE = 84
+
+
+def tile_rows_gmlp_none_kernel(tc, x, w1, hs, w2, out):
+    nc = tc.nc
+    with ExitStack() as ctx:
+        sb = ctx.enter_context(tc.tile_pool(name="sb", bufs=1))
+        ps = ctx.enter_context(tc.psum_pool(name="ps", bufs=1))
+        ctx.enter_context(tc.manual_schedule())
+
+        def new(name, shape, dtype):
+            return sb.tile(shape, dtype, name=name, align_bytes=64)
+
+        hbank = [[ps.tile([P, 512], F32, name="hb%d_%d" % (t, i)) for i in range(3)] for t in range(2)]
+        ybank = [ps.tile([P, 512], F32, name="yb%d" % i) for i in range(2)]
+        used = [0, 0]
+
+        def load_rows(name, src, pair, c0, c1):
+            raw = new(name, [P, PACK, c1 - c0], F32)
+            rows = src[2 * pair : 2 * pair + 2].rearrange("g (p j) n -> (g p) j n", j=PACK)
+            nc.sync.dma_start(out=raw[:], in_=rows[:, :, c0:c1])
+            return raw
+
+        def load_w2(name, pair):
+            raw = new(name, [P, 2, PACK, M], F32)
+            nc.sync.dma_start(out=raw[:], in_=w2[2 * pair : 2 * pair + 2].rearrange("g (p j) m -> p g j m", j=PACK))
+            return raw
+
+        def copy_on(eng, o, i):
+            if eng == "v":
+                nc.vector.tensor_copy(out=o, in_=i)
+            else:
+                nc.scalar.copy(out=o, in_=i)
+
+        def cast_x(eng, name, raw, c0, c1):
+            b = new(name, [P, c1 - c0, PACK], BF16)
+            copy_on(eng, b[:].rearrange("p (c i) j -> p c j i", i=4),
+                    raw[:, :, c0:c1].rearrange("p j (c i) -> p c j i", i=4))
+            return b
+
+        def cast_w1(eng, b, raw, s0, s1):
+            copy_on(eng, b[:, :, s0:s1, :].rearrange("p r s j -> p s j r"),
+                    raw[:, :, PACK * s0 : PACK * s1].rearrange("p j (s r) -> p s j r", r=PACK))
+
+        def cast_w2(eng, name, raw):
+            b = new(name, [P, 2, M, PACK], BF16)
+            copy_on(eng, b[:].rearrange("p g (c i) j -> p g c j i", i=4),
+                    raw[:].rearrange("p g j (c i) -> p g c j i", i=4))
+            return b
+
+        def quant(name, flat):
+            words = flat.shape[1] // PACK
+            codes = new(name + "c", [P, words], U32)
+            scales = new(name + "s", [P, words], U8)
+            nc.vector.quantize_mx(out=codes[:].bitcast(FP8X4), scales=scales[:], in_=flat)
+            return codes, scales
+
+        def mm(o, lhs, l0, rhs, r0, rows):
+            nc.tensor.matmul_mx(
+                out=o,
+                lhsT=lhs[0][rows, l0 : l0 + CH].bitcast(FP8X4),
+                lhsT_scale=lhs[1][rows, l0 : l0 + CH],
+                rhs=rhs[0][rows, r0 : r0 + CH].bitcast(FP8X4),
+                rhs_scale=rhs[1][rows, r0 : r0 + CH],
+                start=True,
+                stop=True,
+            )
+
+        def take_bank(t):
+            bank = hbank[t][used[t] % 3]
+            used[t] = used[t] + 1
+            return bank
+
+        def h_a(t, wq, xq, x0):
+            bank = take_bank(t)
+            rows = slice(ROWS * t, ROWS * t + ROWS)
+            for r in range(PACK):
+                mm(bank[:, CH * r : CH * r + CH], wq, CH * r, xq, x0, rows)
+            return bank
+
+        def h_b(t, wq, xq, r0):
+            bank = take_bank(t)
+            rows = slice(ROWS * t, ROWS * t + ROWS)
+            for r in range(2):
+                for c in range(2):
+                    mm(bank[:, 256 * r + CH * c : 256 * r + CH * c + CH], wq, CH * (r0 + r), xq, CH * c, rows)
+            return bank
+
+        def e_a(dst, bank, g):
+            nc.vector.tensor_tensor(
+                out=dst,
+                in0=bank[:].rearrange("p (r n) -> p n r", r=PACK),
+                in1=hs_sb[:, g, 0:PACK].unsqueeze(1).to_broadcast([P, CH, PACK]),
+                op=MULT,
+            )
+
+        def e_b(planes, bank, g, r0):
+            for r in range(2):
+                nc.scalar.activation(out=planes[:, r0 + r, :], in_=bank[:, 256 * r : 256 * r + 256], func=COPY,
+                                     scale=hs_sb[:, g, r0 + r : r0 + r + 1])
+
+        def inter(name, planes):
+            b = new(name, [P, 256, PACK], BF16)
+            nc.vector.tensor_copy(out=b[:].rearrange("p (c i) j -> p c j i", i=4),
+                                  in_=planes[:].rearrange("p j (c i) -> p c j i", i=4))
+            return b
+
+        def y_mm(bank, col, w2q, gi, hq, h0):
+            mm(bank[:, col : col + CH], w2q, M * gi, hq, h0, slice(0, P))
+
+        def emit(eng, name, bank, b0, g, c0, c1):
+            o = new(name, [P, c1 - c0], F32)
+            copy_on(eng, o[:], bank[:, b0 : b0 + c1 - c0])
+            nc.sync.dma_start(out=out[g, :, c0:c1], in_=o[:])
+
+        def flat3(b):
+            return b[:].rearrange("p n j -> p (n j)")
+
+        def flat4(b):
+            return b[:].rearrange("p a n j -> p (a n j)")
+
+        w1r0 = load_rows("w1r0", w1, 0, 0, K)
+        x0c0 = load_rows("x0c0", x, 0, 0, 128)
+        hs_sb = new("hs_sb", [P, G, 8], F32)
+        nc.sync.dma_start(out=hs_sb[:, :, 0:PACK], in_=hs.rearrange("g (s r) o -> s g (r o)", r=PACK))
+        x0c1 = load_rows("x0c1", x, 0, 128, 256)
+        x0h1 = load_rows("x0h1", x, 0, 256, 512)
+        w1r1 = load_rows("w1r1", w1, 1, 0, K)
+        x1r = load_rows("x1r", x, 1, 0, N)
+        w2r0 = load_w2("w2r0", 0)
+        w2r1 = load_w2("w2r1", 1)
+
+        w1b0 = new("w1b0", [P, PACK, 128, PACK], BF16)
+        cast_w1("v", w1b0, w1r0, 0, W1_VECTOR_SHARE)
+        cast_w1("s", w1b0, w1r0, W1_VECTOR_SHARE, 128)
+        xb = cast_x("s", "xb0c0", x0c0, 0, 128)
+        w1q0 = quant("w1q0", flat4(w1b0))
+        xq00 = quant("xq00", flat3(xb))
+        bk = {}
+        bk[0] = h_a(0, w1q0, xq00, 0)
+        bk[1] = h_a(1, w1q0, xq00, 0)
+        xb = cast_x("s", "xb0c1", x0c1, 0, 128)
+        xq01 = quant("xq01", flat3(xb))
+        bk[2] = h_a(0, w1q0, xq01, 0)
+        bk[3] = h_a(1, w1q0, xq01, 0)
+        xb0h1 = cast_x("s", "xb0h1", x0h1, 0, 256)
+        w1b1 = new("w1b1", [P, PACK, 128, PACK], BF16)
+        cast_w1("s", w1b1, w1r1, 0, 128)
+
+        hb = [new("hb0c%d" % c, [P, 2, CH, PACK], BF16) for c in range(4)]
+        hq = {}
+        e_a(hb[0][:, 0], bk[0], 0)
+        e_a(hb[0][:, 1], bk[1], 1)
+        e_a(hb[1][:, 0], bk[2], 0)
+        xq0h1 = quant("xq0h1", flat3(xb0h1))
+        bk[4] = h_a(0, w1q0, xq0h1, 0)
+        bk[5] = h_a(1, w1q0, xq0h1, 0)
+        bk[6] = h_a(0, w1q0, xq0h1, 128)
+        bk[7] = h_a(1, w1q0, xq0h1, 128)
+        hq[0] = quant("hq0c0", flat4(hb[0]))
+        e_a(hb[1][:, 1], bk[3], 1)
+        e_a(hb[2][:, 0], bk[4], 0)
+        hq[1] = quant("hq0c1", flat4(hb[1]))
+        e_a(hb[2][:, 1], bk[5], 1)
+        xb1h0 = cast_x("v", "xb1h0", x1r, 0, 256)
+        xb1h1 = cast_x("s", "xb1h1", x1r, 256, 512)
+        w2b0 = cast_w2("s", "w2b0", w2r0)
+        e_a(hb[3][:, 0], bk[6], 0)
+        w1q1 = quant("w1q1", flat4(w1b1))
+        xq1h0 = quant("xq1h0", flat3(xb1h0))
+        a0 = h_a(0, w1q1, xq1h0, 0)
+        b00 = h_b(1, w1q1, xq1h0, 0)
+        a1 = h_a(0, w1q1, xq1h0, 128)
+        b01 = h_b(1, w1q1, xq1h0, 2)
+        e_a(hb[3][:, 1], bk[7], 1)
+        hq[2] = quant("hq0c2", flat4(hb[2]))
+        xq1h1 = quant("xq1h1", flat3(xb1h1))
+        hq[3] = quant("hq0c3", flat4(hb[3]))
+        w2q0 = quant("w2q0", flat4(w2b0))
+        a2 = h_a(0, w1q1, xq1h1, 0)
+        b10 = h_b(1, w1q1, xq1h1, 0)
+        for gi in range(2):
+            for c in range(4):
+                y_mm(ybank[gi], CH * c, w2q0, gi, hq[c], CH * gi)
+        pl0 = new("pl0", [P, PACK, 256], BF16)
+        e_b(pl0, b00, 3, 0)
+        e_b(pl0, b01, 3, 2)
+        h2a = new("h2a", [P, 2, CH, PACK], BF16)
+        e_a(h2a[:, 0], a0, 2)
+        e_a(h2a[:, 1], a1, 2)
+        a3 = h_a(0, w1q1, xq1h1, 128)
+        b11 = h_b(1, w1q1, xq1h1, 2)
+        emit("s", "o0", ybank[0], 0, 0, 0, N)
+        emit("s", "o1", ybank[1], 0, 1, 0, N)
+        w2b1 = cast_w2("s", "w2b1", w2r1)
+        h3a = inter("h3a", pl0)
+        hq2a = quant("hq2a", flat4(h2a))
+        h2c2 = new("h2c2", [P, CH, PACK], BF16)
+        e_a(h2c2[:], a2, 2)
+        hq3a = quant("hq3a", flat3(h3a))
+        pl1 = new("pl1", [P, PACK, 256], BF16)
+        e_b(pl1, b10, 3, 0)
+        e_b(pl1, b11, 3, 2)
+        w2q1 = quant("w2q1", flat4(w2b1))
+        hq2c2 = quant("hq2c2", flat3(h2c2))
+        y_mm(ybank[0], 0, w2q1, 0, hq2a, 0)
+        y_mm(ybank[0], CH, w2q1, 0, hq2a, CH)
+        y_mm(ybank[0], 2 * CH, w2q1, 0, hq2c2, 0)
+        y_mm(ybank[1], 0, w2q1, 1, hq3a, 0)
+        y_mm(ybank[1], CH, w2q1, 1, hq3a, CH)
+        h2c3 = new("h2c3", [P, CH, PACK], BF16)
+        e_a(h2c3[:], a3, 2)
+        h3b = inter("h3b", pl1)
+        emit("s", "o2a", ybank[0], 0, 2, 0, 384)
+        emit("s", "o3a", ybank[1], 0, 3, 0, 256)
+        hq2c3 = quant("hq2c3", flat3(h2c3))
+        hq3b = quant("hq3b", flat3(h3b))
+        y_mm(ybank[0], 3 * CH, w2q1, 0, hq2c3, 0)
+        y_mm(ybank[1], 2 * CH, w2q1, 1, hq3b, 0)
+        y_mm(ybank[1], 3 * CH, w2q1, 1, hq3b, CH)
+        emit("s", "o2b", ybank[0], 384, 2, 384, N)
+        emit("v", "o3b", ybank[1], 256, 3, 256, N)

@@ -10,232 +10,226 @@ BF16 = mybir.dt.bfloat16
 U32 = mybir.dt.uint32
 U8 = mybir.dt.uint8
 FP8X4 = mybir.dt.float8_e4m3fn_x4
-MULT = mybir.AluOpType.mult
-COPY = mybir.ActivationFunctionType.Copy
 
 P = 128
-ROWS = 64
 PACK = 4
-CH = 128
-W1_VECTOR_SHARE = 84
+ROWS = D // PACK
+CHUNK = 128
+HALF = N // 2
+RUN = 4
+Z_BANKS = 3
+HS_PITCH = 8
+W1_SPLIT_FIRST = 84
+W1_SPLIT_SECOND = 44
 
 
 def tile_rows_gmlp_none_kernel(tc, x, w1, hs, w2, out):
     nc = tc.nc
+    on_vector = nc.vector.tensor_copy
+    on_scalar = nc.scalar.copy
     with ExitStack() as ctx:
-        sb = ctx.enter_context(tc.tile_pool(name="sb", bufs=1))
-        ps = ctx.enter_context(tc.psum_pool(name="ps", bufs=1))
+        sbuf = ctx.enter_context(tc.tile_pool(name="sbuf", bufs=1))
+        psum = ctx.enter_context(tc.psum_pool(name="psum", bufs=1))
         ctx.enter_context(tc.manual_schedule())
 
+        z_banks = [
+            [psum.tile([P, PACK * CHUNK], F32, name="z%d_%d" % (c, i)) for i in range(Z_BANKS)]
+            for c in range(2)
+        ]
+        y_banks = [psum.tile([P, N], F32, name="y%d" % i) for i in range(2)]
+
         def new(name, shape, dtype):
-            return sb.tile(shape, dtype, name=name, align_bytes=64)
+            return sbuf.tile(shape, dtype, name=name, align_bytes=64)
 
-        hbank = [[ps.tile([P, 512], F32, name="hb%d_%d" % (t, i)) for i in range(3)] for t in range(2)]
-        ybank = [ps.tile([P, 512], F32, name="yb%d" % i) for i in range(2)]
-        used = [0, 0]
-
-        def load_rows(name, src, pair, c0, c1):
-            raw = new(name, [P, PACK, c1 - c0], F32)
+        def load_features(name, src, pair, j0, j1):
+            raw = new(name, [P, j1 - j0, src.shape[2]], F32)
             rows = src[2 * pair : 2 * pair + 2].rearrange("g (p j) n -> (g p) j n", j=PACK)
-            nc.sync.dma_start(out=raw[:], in_=rows[:, :, c0:c1])
+            nc.sync.dma_start(out=raw[:], in_=rows[:, j0:j1, :])
             return raw
 
         def load_w2(name, pair):
             raw = new(name, [P, 2, PACK, M], F32)
-            nc.sync.dma_start(out=raw[:], in_=w2[2 * pair : 2 * pair + 2].rearrange("g (p j) m -> p g j m", j=PACK))
+            rows = w2[2 * pair : 2 * pair + 2].rearrange("g (s r) m -> s g r m", r=PACK)
+            nc.sync.dma_start(out=raw[:], in_=rows)
             return raw
 
-        def copy_on(eng, o, i):
-            if eng == "v":
-                nc.vector.tensor_copy(out=o, in_=i)
-            else:
-                nc.scalar.copy(out=o, in_=i)
+        def interleave(copy, dst, src):
+            copy(
+                out=dst.rearrange("p (a i) j -> p a j i", i=RUN),
+                in_=src.rearrange("p j (a i) -> p a j i", i=RUN),
+            )
 
-        def cast_x(eng, name, raw, c0, c1):
-            b = new(name, [P, c1 - c0, PACK], BF16)
-            copy_on(eng, b[:].rearrange("p (c i) j -> p c j i", i=4),
-                    raw[:, :, c0:c1].rearrange("p j (c i) -> p c j i", i=4))
-            return b
+        def round_w1(copy, dst, raw, j0, s0, s1):
+            j1 = j0 + raw.shape[1]
+            copy(
+                out=dst[:, :, s0:s1, j0:j1].rearrange("p r s j -> p s j r"),
+                in_=raw[:, :, PACK * s0 : PACK * s1].rearrange("p j (s r) -> p s j r", r=PACK),
+            )
 
-        def cast_w1(eng, b, raw, s0, s1):
-            copy_on(eng, b[:, :, s0:s1, :].rearrange("p r s j -> p s j r"),
-                    raw[:, :, PACK * s0 : PACK * s1].rearrange("p j (s r) -> p s j r", r=PACK))
+        def round_x(name, raw, n0, n1):
+            dst = new(name, [P, n1 - n0, PACK], BF16)
+            interleave(on_scalar, dst[:], raw[:, :, n0:n1])
+            return dst
 
-        def cast_w2(eng, name, raw):
-            b = new(name, [P, 2, M, PACK], BF16)
-            copy_on(eng, b[:].rearrange("p g (c i) j -> p g c j i", i=4),
-                    raw[:].rearrange("p g j (c i) -> p g c j i", i=4))
-            return b
+        def round_w2(name, raw):
+            dst = new(name, [P, 2, M, PACK], BF16)
+            on_scalar(
+                out=dst[:].rearrange("p g (a i) r -> p g a r i", i=RUN),
+                in_=raw[:].rearrange("p g r (a i) -> p g a r i", i=RUN),
+            )
+            return dst
 
-        def quant(name, flat):
-            words = flat.shape[1] // PACK
-            codes = new(name + "c", [P, words], U32)
-            scales = new(name + "s", [P, words], U8)
-            nc.vector.quantize_mx(out=codes[:].bitcast(FP8X4), scales=scales[:], in_=flat)
-            return codes, scales
+        def quantise(name, values):
+            pattern = "p a j -> p (a j)" if values.ndim == 3 else "p a b j -> p (a b j)"
+            flat = values.rearrange(pattern)
+            width = flat.shape[1] // PACK
+            words = new(name + "_words", [P, width], U32)
+            scales = new(name + "_scales", [P, width], U8)
+            nc.vector.quantize_mx(out=words[:].bitcast(FP8X4), scales=scales[:], in_=flat)
+            return words, scales
 
-        def mm(o, lhs, l0, rhs, r0, rows):
+        def matmul(dst, rows, stationary, s_block, moving, m_block):
+            s_cols = slice(CHUNK * s_block, CHUNK * (s_block + 1))
+            m_cols = slice(CHUNK * m_block, CHUNK * (m_block + 1))
             nc.tensor.matmul_mx(
-                out=o,
-                lhsT=lhs[0][rows, l0 : l0 + CH].bitcast(FP8X4),
-                lhsT_scale=lhs[1][rows, l0 : l0 + CH],
-                rhs=rhs[0][rows, r0 : r0 + CH].bitcast(FP8X4),
-                rhs_scale=rhs[1][rows, r0 : r0 + CH],
+                out=dst,
+                lhsT=stationary[0][rows, s_cols].bitcast(FP8X4),
+                lhsT_scale=stationary[1][rows, s_cols],
+                rhs=moving[0][rows, m_cols].bitcast(FP8X4),
+                rhs_scale=moving[1][rows, m_cols],
                 start=True,
                 stop=True,
             )
 
-        def take_bank(t):
-            bank = hbank[t][used[t] % 3]
-            used[t] = used[t] + 1
-            return bank
-
-        def h_a(t, wq, xq, x0):
-            bank = take_bank(t)
-            rows = slice(ROWS * t, ROWS * t + ROWS)
+        def first_layer(step, w1_q, x_q, x_block):
+            banks = [z_banks[c][step % Z_BANKS] for c in range(2)]
             for r in range(PACK):
-                mm(bank[:, CH * r : CH * r + CH], wq, CH * r, xq, x0, rows)
-            return bank
-
-        def h_b(t, wq, xq, r0):
-            bank = take_bank(t)
-            rows = slice(ROWS * t, ROWS * t + ROWS)
-            for r in range(2):
                 for c in range(2):
-                    mm(bank[:, 256 * r + CH * c : 256 * r + CH * c + CH], wq, CH * (r0 + r), xq, CH * c, rows)
-            return bank
+                    rows = slice(ROWS * c, ROWS * (c + 1))
+                    matmul(banks[c][:, CHUNK * r : CHUNK * (r + 1)], rows, w1_q, r, x_q, x_block)
+            return banks
 
-        def e_a(dst, bank, g):
+        def second_layer(bank, place, w2_q, c, h_q, h_block):
+            matmul(bank[:, CHUNK * place : CHUNK * (place + 1)], slice(0, P), w2_q, c, h_q, h_block)
+
+        def scale_on_vector(dst, bank, g):
             nc.vector.tensor_tensor(
                 out=dst,
                 in0=bank[:].rearrange("p (r n) -> p n r", r=PACK),
-                in1=hs_sb[:, g, 0:PACK].unsqueeze(1).to_broadcast([P, CH, PACK]),
-                op=MULT,
+                in1=hs_sb[:, g, 0:PACK].unsqueeze(1).to_broadcast([P, CHUNK, PACK]),
+                op=mybir.AluOpType.mult,
             )
 
-        def e_b(planes, bank, g, r0):
-            for r in range(2):
-                nc.scalar.activation(out=planes[:, r0 + r, :], in_=bank[:, 256 * r : 256 * r + 256], func=COPY,
-                                     scale=hs_sb[:, g, r0 + r : r0 + r + 1])
+        def scale_on_scalar(name, bank, g):
+            dst = new(name, [P, PACK, CHUNK], BF16)
+            for r in range(PACK):
+                nc.scalar.activation(
+                    out=dst[:, r, :],
+                    in_=bank[:, CHUNK * r : CHUNK * (r + 1)],
+                    func=mybir.ActivationFunctionType.Copy,
+                    scale=hs_sb[:, g, r : r + 1],
+                )
+            return dst
 
-        def inter(name, planes):
-            b = new(name, [P, 256, PACK], BF16)
-            nc.vector.tensor_copy(out=b[:].rearrange("p (c i) j -> p c j i", i=4),
-                                  in_=planes[:].rearrange("p j (c i) -> p c j i", i=4))
-            return b
+        def store(copy, name, bank, g, n0, n1):
+            result = new(name, [P, n1 - n0], F32)
+            copy(out=result[:], in_=bank[:, 0 : n1 - n0])
+            nc.sync.dma_start(out=out[g, :, n0:n1], in_=result[:])
 
-        def y_mm(bank, col, w2q, gi, hq, h0):
-            mm(bank[:, col : col + CH], w2q, M * gi, hq, h0, slice(0, P))
-
-        def emit(eng, name, bank, b0, g, c0, c1):
-            o = new(name, [P, c1 - c0], F32)
-            copy_on(eng, o[:], bank[:, b0 : b0 + c1 - c0])
-            nc.sync.dma_start(out=out[g, :, c0:c1], in_=o[:])
-
-        def flat3(b):
-            return b[:].rearrange("p n j -> p (n j)")
-
-        def flat4(b):
-            return b[:].rearrange("p a n j -> p (a n j)")
-
-        w1r0 = load_rows("w1r0", w1, 0, 0, K)
-        x0c0 = load_rows("x0c0", x, 0, 0, 128)
-        hs_sb = new("hs_sb", [P, G, 8], F32)
+        w1_raw0 = [load_features("w1_raw0_%d" % j0, w1, 0, j0, j0 + 2) for j0 in (0, 2)]
+        x_raw0 = [load_features("x_raw0_%d" % j0, x, 0, j0, j0 + 2) for j0 in (0, 2)]
+        hs_sb = new("hs_sb", [P, G, HS_PITCH], F32)
         nc.sync.dma_start(out=hs_sb[:, :, 0:PACK], in_=hs.rearrange("g (s r) o -> s g (r o)", r=PACK))
-        x0c1 = load_rows("x0c1", x, 0, 128, 256)
-        x0h1 = load_rows("x0h1", x, 0, 256, 512)
-        w1r1 = load_rows("w1r1", w1, 1, 0, K)
-        x1r = load_rows("x1r", x, 1, 0, N)
-        w2r0 = load_w2("w2r0", 0)
-        w2r1 = load_w2("w2r1", 1)
+        w1_raw1 = load_features("w1_raw1", w1, 1, 0, PACK)
+        x_raw1 = load_features("x_raw1", x, 1, 0, PACK)
+        w2_raw = [load_w2("w2_raw%d" % pair, pair) for pair in range(2)]
 
-        w1b0 = new("w1b0", [P, PACK, 128, PACK], BF16)
-        cast_w1("v", w1b0, w1r0, 0, W1_VECTOR_SHARE)
-        cast_w1("s", w1b0, w1r0, W1_VECTOR_SHARE, 128)
-        xb = cast_x("s", "xb0c0", x0c0, 0, 128)
-        w1q0 = quant("w1q0", flat4(w1b0))
-        xq00 = quant("xq00", flat3(xb))
-        bk = {}
-        bk[0] = h_a(0, w1q0, xq00, 0)
-        bk[1] = h_a(1, w1q0, xq00, 0)
-        xb = cast_x("s", "xb0c1", x0c1, 0, 128)
-        xq01 = quant("xq01", flat3(xb))
-        bk[2] = h_a(0, w1q0, xq01, 0)
-        bk[3] = h_a(1, w1q0, xq01, 0)
-        xb0h1 = cast_x("s", "xb0h1", x0h1, 0, 256)
-        w1b1 = new("w1b1", [P, PACK, 128, PACK], BF16)
-        cast_w1("s", w1b1, w1r1, 0, 128)
+        w1_bf0 = new("w1_bf0", [P, PACK, CHUNK, PACK], BF16)
+        for half in range(2):
+            round_w1(on_vector, w1_bf0, w1_raw0[half], 2 * half, 0, W1_SPLIT_FIRST)
+            round_w1(on_scalar, w1_bf0, w1_raw0[half], 2 * half, W1_SPLIT_FIRST, CHUNK)
+        w1_q0 = quantise("w1_q0", w1_bf0[:])
+        x_bf0 = [new("x_bf0_%d" % i, [P, width, PACK], BF16) for i, width in enumerate((CHUNK, CHUNK, HALF))]
+        for half in range(2):
+            places = slice(2 * half, 2 * half + 2)
+            interleave(on_vector, x_bf0[0][:, :, places], x_raw0[half][:, :, 0:CHUNK])
+            interleave(on_vector, x_bf0[1][:, :, places], x_raw0[half][:, :, CHUNK:HALF])
+            interleave(on_scalar, x_bf0[2][:, :, places], x_raw0[half][:, :, HALF:N])
+        x_q = quantise("x_q0_0", x_bf0[0][:])
+        z0 = first_layer(0, w1_q0, x_q, 0)
+        x_q = quantise("x_q0_1", x_bf0[1][:])
+        z1 = first_layer(1, w1_q0, x_q, 0)
+        x_q = quantise("x_q0_23", x_bf0[2][:])
+        z2 = first_layer(2, w1_q0, x_q, 0)
 
-        hb = [new("hb0c%d" % c, [P, 2, CH, PACK], BF16) for c in range(4)]
-        hq = {}
-        e_a(hb[0][:, 0], bk[0], 0)
-        e_a(hb[0][:, 1], bk[1], 1)
-        e_a(hb[1][:, 0], bk[2], 0)
-        xq0h1 = quant("xq0h1", flat3(xb0h1))
-        bk[4] = h_a(0, w1q0, xq0h1, 0)
-        bk[5] = h_a(1, w1q0, xq0h1, 0)
-        bk[6] = h_a(0, w1q0, xq0h1, 128)
-        bk[7] = h_a(1, w1q0, xq0h1, 128)
-        hq[0] = quant("hq0c0", flat4(hb[0]))
-        e_a(hb[1][:, 1], bk[3], 1)
-        e_a(hb[2][:, 0], bk[4], 0)
-        hq[1] = quant("hq0c1", flat4(hb[1]))
-        e_a(hb[2][:, 1], bk[5], 1)
-        xb1h0 = cast_x("v", "xb1h0", x1r, 0, 256)
-        xb1h1 = cast_x("s", "xb1h1", x1r, 256, 512)
-        w2b0 = cast_w2("s", "w2b0", w2r0)
-        e_a(hb[3][:, 0], bk[6], 0)
-        w1q1 = quant("w1q1", flat4(w1b1))
-        xq1h0 = quant("xq1h0", flat3(xb1h0))
-        a0 = h_a(0, w1q1, xq1h0, 0)
-        b00 = h_b(1, w1q1, xq1h0, 0)
-        a1 = h_a(0, w1q1, xq1h0, 128)
-        b01 = h_b(1, w1q1, xq1h0, 2)
-        e_a(hb[3][:, 1], bk[7], 1)
-        hq[2] = quant("hq0c2", flat4(hb[2]))
-        xq1h1 = quant("xq1h1", flat3(xb1h1))
-        hq[3] = quant("hq0c3", flat4(hb[3]))
-        w2q0 = quant("w2q0", flat4(w2b0))
-        a2 = h_a(0, w1q1, xq1h1, 0)
-        b10 = h_b(1, w1q1, xq1h1, 0)
-        for gi in range(2):
-            for c in range(4):
-                y_mm(ybank[gi], CH * c, w2q0, gi, hq[c], CH * gi)
-        pl0 = new("pl0", [P, PACK, 256], BF16)
-        e_b(pl0, b00, 3, 0)
-        e_b(pl0, b01, 3, 2)
-        h2a = new("h2a", [P, 2, CH, PACK], BF16)
-        e_a(h2a[:, 0], a0, 2)
-        e_a(h2a[:, 1], a1, 2)
-        a3 = h_a(0, w1q1, xq1h1, 128)
-        b11 = h_b(1, w1q1, xq1h1, 2)
-        emit("s", "o0", ybank[0], 0, 0, 0, N)
-        emit("s", "o1", ybank[1], 0, 1, 0, N)
-        w2b1 = cast_w2("s", "w2b1", w2r1)
-        h3a = inter("h3a", pl0)
-        hq2a = quant("hq2a", flat4(h2a))
-        h2c2 = new("h2c2", [P, CH, PACK], BF16)
-        e_a(h2c2[:], a2, 2)
-        hq3a = quant("hq3a", flat3(h3a))
-        pl1 = new("pl1", [P, PACK, 256], BF16)
-        e_b(pl1, b10, 3, 0)
-        e_b(pl1, b11, 3, 2)
-        w2q1 = quant("w2q1", flat4(w2b1))
-        hq2c2 = quant("hq2c2", flat3(h2c2))
-        y_mm(ybank[0], 0, w2q1, 0, hq2a, 0)
-        y_mm(ybank[0], CH, w2q1, 0, hq2a, CH)
-        y_mm(ybank[0], 2 * CH, w2q1, 0, hq2c2, 0)
-        y_mm(ybank[1], 0, w2q1, 1, hq3a, 0)
-        y_mm(ybank[1], CH, w2q1, 1, hq3a, CH)
-        h2c3 = new("h2c3", [P, CH, PACK], BF16)
-        e_a(h2c3[:], a3, 2)
-        h3b = inter("h3b", pl1)
-        emit("s", "o2a", ybank[0], 0, 2, 0, 384)
-        emit("s", "o3a", ybank[1], 0, 3, 0, 256)
-        hq2c3 = quant("hq2c3", flat3(h2c3))
-        hq3b = quant("hq3b", flat3(h3b))
-        y_mm(ybank[0], 3 * CH, w2q1, 0, hq2c3, 0)
-        y_mm(ybank[1], 2 * CH, w2q1, 1, hq3b, 0)
-        y_mm(ybank[1], 3 * CH, w2q1, 1, hq3b, CH)
-        emit("s", "o2b", ybank[0], 384, 2, 384, N)
-        emit("v", "o3b", ybank[1], 256, 3, 256, N)
+        h01 = [new("h01_%d" % i, [P, 2, CHUNK, PACK], BF16) for i in range(4)]
+        h2 = [new("h2_%d" % i, [P, 2, CHUNK, PACK], BF16) for i in range(2)]
+        h3 = [new("h3_%d" % i, [P, 2, CHUNK, PACK], BF16) for i in range(2)]
+        h01_q = []
+
+        scale_on_vector(h01[0][:, 0], z0[0], 0)
+        scaled_1_0 = scale_on_scalar("scaled_1_0", z0[1], 1)
+        z3 = first_layer(3, w1_q0, x_q, 1)
+        scaled_1_1 = scale_on_scalar("scaled_1_1", z1[1], 1)
+        w1_bf1 = new("w1_bf1", [P, PACK, CHUNK, PACK], BF16)
+        round_w1(on_scalar, w1_bf1, w1_raw1, 0, W1_SPLIT_SECOND, CHUNK)
+        scale_on_vector(h01[1][:, 0], z1[0], 0)
+        interleave(on_vector, h01[0][:, 1], scaled_1_0[:])
+        scale_on_vector(h01[2][:, 0], z2[0], 0)
+        interleave(on_vector, h01[1][:, 1], scaled_1_1[:])
+        h01_q.append(quantise("h01_q0", h01[0][:]))
+        scale_on_vector(h01[2][:, 1], z2[1], 1)
+
+        round_w1(on_vector, w1_bf1, w1_raw1, 0, 0, W1_SPLIT_SECOND)
+        x_bf1_0 = round_x("x_bf1_0", x_raw1, 0, CHUNK)
+        x_bf1_1 = round_x("x_bf1_1", x_raw1, CHUNK, HALF)
+        x_bf1_23 = round_x("x_bf1_23", x_raw1, HALF, N)
+        w2_bf0 = round_w2("w2_bf0", w2_raw[0])
+        h01_q.append(quantise("h01_q1", h01[1][:]))
+        w1_q1 = quantise("w1_q1", w1_bf1[:])
+        x_q = quantise("x_q1_0", x_bf1_0[:])
+        z4 = first_layer(4, w1_q1, x_q, 0)
+        scale_on_vector(h01[3][:, 0], z3[0], 0)
+        x_q = quantise("x_q1_1", x_bf1_1[:])
+        z5 = first_layer(5, w1_q1, x_q, 0)
+        scale_on_vector(h01[3][:, 1], z3[1], 1)
+        h01_q.append(quantise("h01_q2", h01[2][:]))
+        scale_on_vector(h2[0][:, 0], z4[0], 2)
+        x_q = quantise("x_q1_23", x_bf1_23[:])
+        z6 = first_layer(6, w1_q1, x_q, 0)
+        scaled_3_0 = scale_on_scalar("scaled_3_0", z4[1], 3)
+        z7 = first_layer(7, w1_q1, x_q, 1)
+        w2_bf1 = round_w2("w2_bf1", w2_raw[1])
+        h01_q.append(quantise("h01_q3", h01[3][:]))
+        scale_on_vector(h2[0][:, 1], z5[0], 2)
+        scale_on_vector(h3[0][:, 1], z5[1], 3)
+
+        w2_q0 = quantise("w2_q0", w2_bf0[:])
+        for c in range(2):
+            for chunk in range(4):
+                second_layer(y_banks[c], chunk, w2_q0, c, h01_q[chunk], c)
+        store(on_scalar, "out_0", y_banks[0], 0, 0, N)
+        scaled_3_3 = scale_on_scalar("scaled_3_3", z7[1], 3)
+        store(on_scalar, "out_1", y_banks[1], 1, 0, N)
+
+        scale_on_vector(h2[1][:, 0], z6[0], 2)
+        interleave(on_vector, h3[0][:, 0], scaled_3_0[:])
+        scale_on_vector(h2[1][:, 1], z7[0], 2)
+        h2_q0 = quantise("h2_q0", h2[0][:])
+        w2_q1 = quantise("w2_q1", w2_bf1[:])
+        h2_q1 = quantise("h2_q1", h2[1][:])
+        h3_q0 = quantise("h3_q0", h3[0][:])
+        for chunk in range(4):
+            second_layer(y_banks[0], chunk, w2_q1, 0, (h2_q0, h2_q1)[chunk // 2], chunk % 2)
+        store(on_scalar, "out_2", y_banks[0], 2, 0, N)
+
+        for chunk in range(2):
+            second_layer(y_banks[1], chunk, w2_q1, 1, h3_q0, chunk)
+        scale_on_vector(h3[1][:, 0], z6[1], 3)
+        interleave(on_vector, h3[1][:, 1], scaled_3_3[:])
+        h3_q2 = quantise("h3_q2", h3[1][:, 0])
+        h3_q3 = quantise("h3_q3", h3[1][:, 1])
+        store(on_scalar, "out_3a", y_banks[1], 3, 0, HALF)
+        second_layer(y_banks[0], 0, w2_q1, 1, h3_q2, 0)
+        second_layer(y_banks[0], 1, w2_q1, 1, h3_q3, 0)
+        store(on_vector, "out_3b", y_banks[0], 3, HALF, N)

@@ -19,8 +19,8 @@ HALF = N // 2
 RUN = 4
 Z_BANKS = 3
 HS_PITCH = 8
-W1_SPLIT_FIRST = 84
-W1_SPLIT_SECOND = 44
+W1_SPLIT = 84
+X_SPLIT = 64
 
 
 def tile_rows_gmlp_none_kernel(tc, x, w1, hs, w2, out):
@@ -41,15 +41,11 @@ def tile_rows_gmlp_none_kernel(tc, x, w1, hs, w2, out):
         def new(name, shape, dtype):
             return sbuf.tile(shape, dtype, name=name, align_bytes=64)
 
-        def load_features(name, src, pair, j0, j1):
-            raw = new(name, [P, j1 - j0, src.shape[2]], F32)
-            rows = src[2 * pair : 2 * pair + 2].rearrange("g (p j) n -> (g p) j n", j=PACK)
-            nc.sync.dma_start(out=raw[:], in_=rows[:, j0:j1, :])
-            return raw
+        def pair_rows(src, pair):
+            return src[2 * pair : 2 * pair + 2].rearrange("g (p j) n -> (g p) j n", j=PACK)
 
-        def load_w2(name, pair):
-            raw = new(name, [P, 2, PACK, M], F32)
-            rows = w2[2 * pair : 2 * pair + 2].rearrange("g (s r) m -> s g r m", r=PACK)
+        def load(name, rows):
+            raw = new(name, list(rows.shape), F32)
             nc.sync.dma_start(out=raw[:], in_=rows)
             return raw
 
@@ -66,9 +62,9 @@ def tile_rows_gmlp_none_kernel(tc, x, w1, hs, w2, out):
                 in_=raw[:, :, PACK * s0 : PACK * s1].rearrange("p j (s r) -> p s j r", r=PACK),
             )
 
-        def round_x(name, raw, n0, n1):
-            dst = new(name, [P, n1 - n0, PACK], BF16)
-            interleave(on_scalar, dst[:], raw[:, :, n0:n1])
+        def round_x(copy, name, raw):
+            dst = new(name, [P, raw.shape[2], PACK], BF16)
+            interleave(copy, dst[:], raw)
             return dst
 
         def round_w2(name, raw):
@@ -131,105 +127,117 @@ def tile_rows_gmlp_none_kernel(tc, x, w1, hs, w2, out):
                 )
             return dst
 
+        def interleave_on_gpsimd(dst, scaled):
+            nc.gpsimd.tensor_scalar(
+                out=dst,
+                in0=scaled[:].rearrange("p r n -> p n r"),
+                scalar1=1.0,
+                scalar2=0.0,
+                op0=mybir.AluOpType.mult,
+                op1=mybir.AluOpType.add,
+            )
+
         def store(copy, name, bank, g, n0, n1):
             result = new(name, [P, n1 - n0], F32)
             copy(out=result[:], in_=bank[:, 0 : n1 - n0])
             nc.sync.dma_start(out=out[g, :, n0:n1], in_=result[:])
 
-        w1_raw0 = [load_features("w1_raw0_%d" % j0, w1, 0, j0, j0 + 2) for j0 in (0, 2)]
-        x_raw0 = [load_features("x_raw0_%d" % j0, x, 0, j0, j0 + 2) for j0 in (0, 2)]
+        w1_raw0 = [load("w1_raw0_%d" % j0, pair_rows(w1, 0)[:, j0 : j0 + 2, :]) for j0 in (0, 2)]
+        x_raw0_0 = load("x_raw0_0", pair_rows(x, 0)[:, :, 0:CHUNK])
+        x_raw0_1 = load("x_raw0_1", pair_rows(x, 0)[:, :, CHUNK:HALF])
         hs_sb = new("hs_sb", [P, G, HS_PITCH], F32)
         nc.sync.dma_start(out=hs_sb[:, :, 0:PACK], in_=hs.rearrange("g (s r) o -> s g (r o)", r=PACK))
-        w1_raw1 = load_features("w1_raw1", w1, 1, 0, PACK)
-        x_raw1 = load_features("x_raw1", x, 1, 0, PACK)
-        w2_raw = [load_w2("w2_raw%d" % pair, pair) for pair in range(2)]
+        x_raw0_23 = load("x_raw0_23", pair_rows(x, 0)[:, :, HALF:N])
+        w1_raw1 = load("w1_raw1", pair_rows(w1, 1))
+        x_raw1 = load("x_raw1", pair_rows(x, 1))
+        w2_raw = [
+            load("w2_raw%d" % pair, w2[2 * pair : 2 * pair + 2].rearrange("g (s r) m -> s g r m", r=PACK))
+            for pair in range(2)
+        ]
 
         w1_bf0 = new("w1_bf0", [P, PACK, CHUNK, PACK], BF16)
         for half in range(2):
-            round_w1(on_vector, w1_bf0, w1_raw0[half], 2 * half, 0, W1_SPLIT_FIRST)
-            round_w1(on_scalar, w1_bf0, w1_raw0[half], 2 * half, W1_SPLIT_FIRST, CHUNK)
+            round_w1(on_vector, w1_bf0, w1_raw0[half], 2 * half, 0, W1_SPLIT)
+            round_w1(on_scalar, w1_bf0, w1_raw0[half], 2 * half, W1_SPLIT, CHUNK)
+        x_bf0_0 = new("x_bf0_0", [P, CHUNK, PACK], BF16)
+        interleave(on_vector, x_bf0_0[:, 0:X_SPLIT, :], x_raw0_0[:, :, 0:X_SPLIT])
+        interleave(on_scalar, x_bf0_0[:, X_SPLIT:CHUNK, :], x_raw0_0[:, :, X_SPLIT:CHUNK])
+        x_bf0_1 = round_x(on_scalar, "x_bf0_1", x_raw0_1[:])
+        x_bf0_2 = round_x(on_scalar, "x_bf0_2", x_raw0_23[:, :, 0:CHUNK])
+        x_bf0_3 = round_x(on_scalar, "x_bf0_3", x_raw0_23[:, :, CHUNK:HALF])
         w1_q0 = quantise("w1_q0", w1_bf0[:])
-        x_bf0 = [new("x_bf0_%d" % i, [P, width, PACK], BF16) for i, width in enumerate((CHUNK, CHUNK, HALF))]
-        for half in range(2):
-            places = slice(2 * half, 2 * half + 2)
-            interleave(on_vector, x_bf0[0][:, :, places], x_raw0[half][:, :, 0:CHUNK])
-            interleave(on_vector, x_bf0[1][:, :, places], x_raw0[half][:, :, CHUNK:HALF])
-            interleave(on_scalar, x_bf0[2][:, :, places], x_raw0[half][:, :, HALF:N])
-        x_q = quantise("x_q0_0", x_bf0[0][:])
-        z0 = first_layer(0, w1_q0, x_q, 0)
-        x_q = quantise("x_q0_1", x_bf0[1][:])
-        z1 = first_layer(1, w1_q0, x_q, 0)
-        x_q = quantise("x_q0_23", x_bf0[2][:])
-        z2 = first_layer(2, w1_q0, x_q, 0)
+        z0 = first_layer(0, w1_q0, quantise("x_q0_0", x_bf0_0[:]), 0)
+        z1 = first_layer(1, w1_q0, quantise("x_q0_1", x_bf0_1[:]), 0)
 
-        h01 = [new("h01_%d" % i, [P, 2, CHUNK, PACK], BF16) for i in range(4)]
-        h2 = [new("h2_%d" % i, [P, 2, CHUNK, PACK], BF16) for i in range(2)]
-        h3 = [new("h3_%d" % i, [P, 2, CHUNK, PACK], BF16) for i in range(2)]
-        h01_q = []
+        h_q = {}
 
-        scale_on_vector(h01[0][:, 0], z0[0], 0)
-        scaled_1_0 = scale_on_scalar("scaled_1_0", z0[1], 1)
-        z3 = first_layer(3, w1_q0, x_q, 1)
+        def quantise_h(name, values, chunks):
+            quantised = quantise(name, values)
+            for block, key in enumerate(chunks):
+                h_q[key] = (quantised, block)
+
+        h_a = new("h_a", [P, 2, CHUNK, PACK], BF16)
+        h_b = new("h_b", [P, 2, CHUNK, PACK], BF16)
+        h_c = new("h_c", [P, 2, CHUNK, PACK], BF16)
+        scale_on_vector(h_a[:, 0], z0[0], 0)
+        scale_on_vector(h_a[:, 1], z0[1], 1)
+        z2 = first_layer(2, w1_q0, quantise("x_q0_2", x_bf0_2[:]), 0)
+        scale_on_vector(h_b[:, 0], z1[0], 0)
         scaled_1_1 = scale_on_scalar("scaled_1_1", z1[1], 1)
+        z3 = first_layer(3, w1_q0, quantise("x_q0_3", x_bf0_3[:]), 0)
+        quantise_h("h_q_a", h_a[:], [(0, 0), (1, 0)])
+        interleave_on_gpsimd(h_a[:, 1], scaled_1_1)
+        scale_on_vector(h_b[:, 1], z2[0], 0)
+        scale_on_vector(h_a[:, 0], z2[1], 1)
+        quantise_h("h_q_b", h_b[:], [(0, 1), (0, 2)])
+        scale_on_vector(h_c[:, 0], z3[0], 0)
+
         w1_bf1 = new("w1_bf1", [P, PACK, CHUNK, PACK], BF16)
-        round_w1(on_scalar, w1_bf1, w1_raw1, 0, W1_SPLIT_SECOND, CHUNK)
-        scale_on_vector(h01[1][:, 0], z1[0], 0)
-        interleave(on_vector, h01[0][:, 1], scaled_1_0[:])
-        scale_on_vector(h01[2][:, 0], z2[0], 0)
-        interleave(on_vector, h01[1][:, 1], scaled_1_1[:])
-        h01_q.append(quantise("h01_q0", h01[0][:]))
-        scale_on_vector(h01[2][:, 1], z2[1], 1)
-
-        round_w1(on_vector, w1_bf1, w1_raw1, 0, 0, W1_SPLIT_SECOND)
-        x_bf1_0 = round_x("x_bf1_0", x_raw1, 0, CHUNK)
-        x_bf1_1 = round_x("x_bf1_1", x_raw1, CHUNK, HALF)
-        x_bf1_23 = round_x("x_bf1_23", x_raw1, HALF, N)
+        round_w1(on_scalar, w1_bf1, w1_raw1, 0, 0, CHUNK)
+        x_bf1_01 = round_x(on_vector, "x_bf1_01", x_raw1[:, :, 0:HALF])
+        x_bf1_23 = round_x(on_scalar, "x_bf1_23", x_raw1[:, :, HALF:N])
         w2_bf0 = round_w2("w2_bf0", w2_raw[0])
-        h01_q.append(quantise("h01_q1", h01[1][:]))
+        quantise_h("h_q_a2", h_a[:], [(1, 2), (1, 1)])
         w1_q1 = quantise("w1_q1", w1_bf1[:])
-        x_q = quantise("x_q1_0", x_bf1_0[:])
-        z4 = first_layer(4, w1_q1, x_q, 0)
-        scale_on_vector(h01[3][:, 0], z3[0], 0)
-        x_q = quantise("x_q1_1", x_bf1_1[:])
-        z5 = first_layer(5, w1_q1, x_q, 0)
-        scale_on_vector(h01[3][:, 1], z3[1], 1)
-        h01_q.append(quantise("h01_q2", h01[2][:]))
-        scale_on_vector(h2[0][:, 0], z4[0], 2)
-        x_q = quantise("x_q1_23", x_bf1_23[:])
-        z6 = first_layer(6, w1_q1, x_q, 0)
+        x_q1_01 = quantise("x_q1_01", x_bf1_01[:])
+        z4 = first_layer(4, w1_q1, x_q1_01, 0)
+        z5 = first_layer(5, w1_q1, x_q1_01, 1)
+        scale_on_vector(h_c[:, 1], z3[1], 1)
+        x_q1_23 = quantise("x_q1_23", x_bf1_23[:])
+        z6 = first_layer(6, w1_q1, x_q1_23, 0)
+        quantise_h("h_q_c", h_c[:], [(0, 3), (1, 3)])
+        h_2 = new("h_2", [P, 4, CHUNK, PACK], BF16)
+        h_3 = new("h_3", [P, 2, CHUNK, PACK], BF16)
+        scale_on_vector(h_2[:, 0], z4[0], 2)
         scaled_3_0 = scale_on_scalar("scaled_3_0", z4[1], 3)
-        z7 = first_layer(7, w1_q1, x_q, 1)
+        scaled_3_1 = scale_on_scalar("scaled_3_1", z5[1], 3)
         w2_bf1 = round_w2("w2_bf1", w2_raw[1])
-        h01_q.append(quantise("h01_q3", h01[3][:]))
-        scale_on_vector(h2[0][:, 1], z5[0], 2)
-        scale_on_vector(h3[0][:, 1], z5[1], 3)
-
         w2_q0 = quantise("w2_q0", w2_bf0[:])
+        z7 = first_layer(7, w1_q1, x_q1_23, 1)
+
         for c in range(2):
             for chunk in range(4):
-                second_layer(y_banks[c], chunk, w2_q0, c, h01_q[chunk], c)
-        store(on_scalar, "out_0", y_banks[0], 0, 0, N)
-        scaled_3_3 = scale_on_scalar("scaled_3_3", z7[1], 3)
-        store(on_scalar, "out_1", y_banks[1], 1, 0, N)
+                second_layer(y_banks[c], chunk, w2_q0, c, *h_q[c, chunk])
+            store(on_scalar, "out_%d" % c, y_banks[c], c, 0, N)
 
-        scale_on_vector(h2[1][:, 0], z6[0], 2)
-        interleave(on_vector, h3[0][:, 0], scaled_3_0[:])
-        scale_on_vector(h2[1][:, 1], z7[0], 2)
-        h2_q0 = quantise("h2_q0", h2[0][:])
+        interleave_on_gpsimd(w2_bf0[:, 0], scaled_3_0)
+        interleave_on_gpsimd(w2_bf0[:, 1], scaled_3_1)
+        scale_on_vector(h_2[:, 1], z5[0], 2)
+        scale_on_vector(h_2[:, 2], z6[0], 2)
+        scale_on_vector(h_3[:, 0], z6[1], 3)
+        scale_on_vector(h_2[:, 3], z7[0], 2)
+
         w2_q1 = quantise("w2_q1", w2_bf1[:])
-        h2_q1 = quantise("h2_q1", h2[1][:])
-        h3_q0 = quantise("h3_q0", h3[0][:])
+        quantise_h("h_q_2", h_2[:], [(2, chunk) for chunk in range(4)])
         for chunk in range(4):
-            second_layer(y_banks[0], chunk, w2_q1, 0, (h2_q0, h2_q1)[chunk // 2], chunk % 2)
+            second_layer(y_banks[0], chunk, w2_q1, 0, *h_q[2, chunk])
         store(on_scalar, "out_2", y_banks[0], 2, 0, N)
-
-        for chunk in range(2):
-            second_layer(y_banks[1], chunk, w2_q1, 1, h3_q0, chunk)
-        scale_on_vector(h3[1][:, 0], z6[1], 3)
-        interleave(on_vector, h3[1][:, 1], scaled_3_3[:])
-        h3_q2 = quantise("h3_q2", h3[1][:, 0])
-        h3_q3 = quantise("h3_q3", h3[1][:, 1])
-        store(on_scalar, "out_3a", y_banks[1], 3, 0, HALF)
-        second_layer(y_banks[0], 0, w2_q1, 1, h3_q2, 0)
-        second_layer(y_banks[0], 1, w2_q1, 1, h3_q3, 0)
-        store(on_vector, "out_3b", y_banks[0], 3, HALF, N)
+        quantise_h("h_q_3_2", h_3[:, 0], [(3, 2)])
+        quantise_h("h_q_3a", w2_bf0[:], [(3, 0), (3, 1)])
+        for chunk in range(3):
+            second_layer(y_banks[1], chunk, w2_q1, 1, *h_q[3, chunk])
+        store(on_scalar, "out_3a", y_banks[1], 3, 0, 3 * CHUNK)
+        scale_on_vector(h_3[:, 1], z7[1], 3)
+        quantise_h("h_q_3_3", h_3[:, 1], [(3, 3)])
+        second_layer(y_banks[0], 0, w2_q1, 1, *h_q[3, 3])
+        store(on_vector, "out_3b", y_banks[0], 3, 3 * CHUNK, N)

from contextlib import ExitStack

import concourse.mybir as mybir

G, D, K, M, N = 4, 256, 512, 128, 512
FLOPS = 2 * G * D * K * N + 2 * G * K * M * N

F32 = mybir.dt.float32
BF16 = mybir.dt.bfloat16
U32 = mybir.dt.uint32
U8 = mybir.dt.uint8
FP8X4 = mybir.dt.float8_e4m3fn_x4

P = 128
PACK = 4
ROWS = D // PACK
CHUNK = 128
HALF = N // 2
RUN = 4
Z_BANKS = 3
HS_PITCH = 8
W1_SPLIT = 84
X_SPLIT = 64


def tile_rows_gmlp_none_kernel(tc, x, w1, hs, w2, out):
    nc = tc.nc
    on_vector = nc.vector.tensor_copy
    on_scalar = nc.scalar.copy
    with ExitStack() as ctx:
        sbuf = ctx.enter_context(tc.tile_pool(name="sbuf", bufs=1))
        psum = ctx.enter_context(tc.psum_pool(name="psum", bufs=1))
        ctx.enter_context(tc.manual_schedule())

        z_banks = [
            [psum.tile([P, PACK * CHUNK], F32, name="z%d_%d" % (c, i)) for i in range(Z_BANKS)]
            for c in range(2)
        ]
        y_banks = [psum.tile([P, N], F32, name="y%d" % i) for i in range(2)]

        def new(name, shape, dtype):
            return sbuf.tile(shape, dtype, name=name, align_bytes=64)

        def pair_rows(src, pair):
            return src[2 * pair : 2 * pair + 2].rearrange("g (p j) n -> (g p) j n", j=PACK)

        def load(name, rows):
            raw = new(name, list(rows.shape), F32)
            nc.sync.dma_start(out=raw[:], in_=rows)
            return raw

        def interleave(copy, dst, src):
            copy(
                out=dst.rearrange("p (a i) j -> p a j i", i=RUN),
                in_=src.rearrange("p j (a i) -> p a j i", i=RUN),
            )

        def round_w1(copy, dst, raw, j0, s0, s1):
            j1 = j0 + raw.shape[1]
            copy(
                out=dst[:, :, s0:s1, j0:j1].rearrange("p r s j -> p s j r"),
                in_=raw[:, :, PACK * s0 : PACK * s1].rearrange("p j (s r) -> p s j r", r=PACK),
            )

        def round_x(copy, name, raw):
            dst = new(name, [P, raw.shape[2], PACK], BF16)
            interleave(copy, dst[:], raw)
            return dst

        def round_w2(name, raw):
            dst = new(name, [P, 2, M, PACK], BF16)
            on_scalar(
                out=dst[:].rearrange("p g (a i) r -> p g a r i", i=RUN),
                in_=raw[:].rearrange("p g r (a i) -> p g a r i", i=RUN),
            )
            return dst

        def quantise(name, values):
            pattern = "p a j -> p (a j)" if values.ndim == 3 else "p a b j -> p (a b j)"
            flat = values.rearrange(pattern)
            width = flat.shape[1] // PACK
            words = new(name + "_words", [P, width], U32)
            scales = new(name + "_scales", [P, width], U8)
            nc.vector.quantize_mx(out=words[:].bitcast(FP8X4), scales=scales[:], in_=flat)
            return words, scales

        def matmul(dst, rows, stationary, s_block, moving, m_block):
            s_cols = slice(CHUNK * s_block, CHUNK * (s_block + 1))
            m_cols = slice(CHUNK * m_block, CHUNK * (m_block + 1))
            nc.tensor.matmul_mx(
                out=dst,
                lhsT=stationary[0][rows, s_cols].bitcast(FP8X4),
                lhsT_scale=stationary[1][rows, s_cols],
                rhs=moving[0][rows, m_cols].bitcast(FP8X4),
                rhs_scale=moving[1][rows, m_cols],
                start=True,
                stop=True,
            )

        def first_layer(step, w1_q, x_q, x_block):
            banks = [z_banks[c][step % Z_BANKS] for c in range(2)]
            for r in range(PACK):
                for c in range(2):
                    rows = slice(ROWS * c, ROWS * (c + 1))
                    matmul(banks[c][:, CHUNK * r : CHUNK * (r + 1)], rows, w1_q, r, x_q, x_block)
            return banks

        def second_layer(bank, place, w2_q, c, h_q, h_block):
            matmul(bank[:, CHUNK * place : CHUNK * (place + 1)], slice(0, P), w2_q, c, h_q, h_block)

        def scale_on_vector(dst, bank, g):
            nc.vector.tensor_tensor(
                out=dst,
                in0=bank[:].rearrange("p (r n) -> p n r", r=PACK),
                in1=hs_sb[:, g, 0:PACK].unsqueeze(1).to_broadcast([P, CHUNK, PACK]),
                op=mybir.AluOpType.mult,
            )

        def scale_on_scalar(name, bank, g):
            dst = new(name, [P, PACK, CHUNK], BF16)
            for r in range(PACK):
                nc.scalar.activation(
                    out=dst[:, r, :],
                    in_=bank[:, CHUNK * r : CHUNK * (r + 1)],
                    func=mybir.ActivationFunctionType.Copy,
                    scale=hs_sb[:, g, r : r + 1],
                )
            return dst

        def interleave_on_gpsimd(dst, scaled):
            nc.gpsimd.tensor_scalar(
                out=dst,
                in0=scaled[:].rearrange("p r n -> p n r"),
                scalar1=1.0,
                scalar2=0.0,
                op0=mybir.AluOpType.mult,
                op1=mybir.AluOpType.add,
            )

        def store(copy, name, bank, g, n0, n1):
            result = new(name, [P, n1 - n0], F32)
            copy(out=result[:], in_=bank[:, 0 : n1 - n0])
            nc.sync.dma_start(out=out[g, :, n0:n1], in_=result[:])

        w1_raw0 = [load("w1_raw0_%d" % j0, pair_rows(w1, 0)[:, j0 : j0 + 2, :]) for j0 in (0, 2)]
        x_raw0_0 = load("x_raw0_0", pair_rows(x, 0)[:, :, 0:CHUNK])
        x_raw0_1 = load("x_raw0_1", pair_rows(x, 0)[:, :, CHUNK:HALF])
        hs_sb = new("hs_sb", [P, G, HS_PITCH], F32)
        nc.sync.dma_start(out=hs_sb[:, :, 0:PACK], in_=hs.rearrange("g (s r) o -> s g (r o)", r=PACK))
        x_raw0_23 = load("x_raw0_23", pair_rows(x, 0)[:, :, HALF:N])
        w1_raw1 = load("w1_raw1", pair_rows(w1, 1))
        x_raw1 = load("x_raw1", pair_rows(x, 1))
        w2_raw = [
            load("w2_raw%d" % pair, w2[2 * pair : 2 * pair + 2].rearrange("g (s r) m -> s g r m", r=PACK))
            for pair in range(2)
        ]

        w1_bf0 = new("w1_bf0", [P, PACK, CHUNK, PACK], BF16)
        for half in range(2):
            round_w1(on_vector, w1_bf0, w1_raw0[half], 2 * half, 0, W1_SPLIT)
            round_w1(on_scalar, w1_bf0, w1_raw0[half], 2 * half, W1_SPLIT, CHUNK)
        x_bf0_0 = new("x_bf0_0", [P, CHUNK, PACK], BF16)
        interleave(on_vector, x_bf0_0[:, 0:X_SPLIT, :], x_raw0_0[:, :, 0:X_SPLIT])
        interleave(on_scalar, x_bf0_0[:, X_SPLIT:CHUNK, :], x_raw0_0[:, :, X_SPLIT:CHUNK])
        x_bf0_1 = round_x(on_scalar, "x_bf0_1", x_raw0_1[:])
        x_bf0_2 = round_x(on_scalar, "x_bf0_2", x_raw0_23[:, :, 0:CHUNK])
        x_bf0_3 = round_x(on_scalar, "x_bf0_3", x_raw0_23[:, :, CHUNK:HALF])
        w1_q0 = quantise("w1_q0", w1_bf0[:])
        z0 = first_layer(0, w1_q0, quantise("x_q0_0", x_bf0_0[:]), 0)
        z1 = first_layer(1, w1_q0, quantise("x_q0_1", x_bf0_1[:]), 0)

        h_q = {}

        def quantise_h(name, values, chunks):
            quantised = quantise(name, values)
            for block, key in enumerate(chunks):
                h_q[key] = (quantised, block)

        h_a = new("h_a", [P, 2, CHUNK, PACK], BF16)
        h_b = new("h_b", [P, 2, CHUNK, PACK], BF16)
        h_c = new("h_c", [P, 2, CHUNK, PACK], BF16)
        scale_on_vector(h_a[:, 0], z0[0], 0)
        scale_on_vector(h_a[:, 1], z0[1], 1)
        z2 = first_layer(2, w1_q0, quantise("x_q0_2", x_bf0_2[:]), 0)
        scale_on_vector(h_b[:, 0], z1[0], 0)
        scaled_1_1 = scale_on_scalar("scaled_1_1", z1[1], 1)
        z3 = first_layer(3, w1_q0, quantise("x_q0_3", x_bf0_3[:]), 0)
        quantise_h("h_q_a", h_a[:], [(0, 0), (1, 0)])
        interleave_on_gpsimd(h_a[:, 1], scaled_1_1)
        scale_on_vector(h_b[:, 1], z2[0], 0)
        scale_on_vector(h_a[:, 0], z2[1], 1)
        quantise_h("h_q_b", h_b[:], [(0, 1), (0, 2)])
        scale_on_vector(h_c[:, 0], z3[0], 0)

        w1_bf1 = new("w1_bf1", [P, PACK, CHUNK, PACK], BF16)
        round_w1(on_scalar, w1_bf1, w1_raw1, 0, 0, CHUNK)
        x_bf1_01 = round_x(on_vector, "x_bf1_01", x_raw1[:, :, 0:HALF])
        x_bf1_23 = round_x(on_scalar, "x_bf1_23", x_raw1[:, :, HALF:N])
        w2_bf0 = round_w2("w2_bf0", w2_raw[0])
        quantise_h("h_q_a2", h_a[:], [(1, 2), (1, 1)])
        w1_q1 = quantise("w1_q1", w1_bf1[:])
        x_q1_01 = quantise("x_q1_01", x_bf1_01[:])
        z4 = first_layer(4, w1_q1, x_q1_01, 0)
        z5 = first_layer(5, w1_q1, x_q1_01, 1)
        scale_on_vector(h_c[:, 1], z3[1], 1)
        x_q1_23 = quantise("x_q1_23", x_bf1_23[:])
        z6 = first_layer(6, w1_q1, x_q1_23, 0)
        quantise_h("h_q_c", h_c[:], [(0, 3), (1, 3)])
        h_2 = new("h_2", [P, 4, CHUNK, PACK], BF16)
        h_3 = new("h_3", [P, 2, CHUNK, PACK], BF16)
        scale_on_vector(h_2[:, 0], z4[0], 2)
        scaled_3_0 = scale_on_scalar("scaled_3_0", z4[1], 3)
        scaled_3_1 = scale_on_scalar("scaled_3_1", z5[1], 3)
        w2_bf1 = round_w2("w2_bf1", w2_raw[1])
        w2_q0 = quantise("w2_q0", w2_bf0[:])
        z7 = first_layer(7, w1_q1, x_q1_23, 1)

        for c in range(2):
            for chunk in range(4):
                second_layer(y_banks[c], chunk, w2_q0, c, *h_q[c, chunk])
            store(on_scalar, "out_%d" % c, y_banks[c], c, 0, N)

        interleave_on_gpsimd(w2_bf0[:, 0], scaled_3_0)
        interleave_on_gpsimd(w2_bf0[:, 1], scaled_3_1)
        scale_on_vector(h_2[:, 1], z5[0], 2)
        scale_on_vector(h_2[:, 2], z6[0], 2)
        scale_on_vector(h_3[:, 0], z6[1], 3)
        scale_on_vector(h_2[:, 3], z7[0], 2)

        w2_q1 = quantise("w2_q1", w2_bf1[:])
        quantise_h("h_q_2", h_2[:], [(2, chunk) for chunk in range(4)])
        for chunk in range(4):
            second_layer(y_banks[0], chunk, w2_q1, 0, *h_q[2, chunk])
        store(on_scalar, "out_2", y_banks[0], 2, 0, N)
        quantise_h("h_q_3_2", h_3[:, 0], [(3, 2)])
        quantise_h("h_q_3a", w2_bf0[:], [(3, 0), (3, 1)])
        for chunk in range(3):
            second_layer(y_banks[1], chunk, w2_q1, 1, *h_q[3, chunk])
        store(on_scalar, "out_3a", y_banks[1], 3, 0, 3 * CHUNK)
        scale_on_vector(h_3[:, 1], z7[1], 3)
        quantise_h("h_q_3_3", h_3[:, 1], [(3, 3)])
        second_layer(y_banks[0], 0, w2_q1, 1, *h_q[3, 3])
        store(on_vector, "out_3b", y_banks[0], 3, 3 * CHUNK, N)
